import numpy as np
import ml_dtypes


def mxq(x, axis, fmt="e4m3"):
    dtype, down = {"e4m3": (ml_dtypes.float8_e4m3fn, 7), "e5m2": (ml_dtypes.float8_e5m2, 14)}[fmt]
    v = np.moveaxis(np.asarray(x, np.float32).astype(ml_dtypes.bfloat16).astype(np.float64), axis, -1)
    blocks = v.reshape(v.shape[:-1] + (-1, 32))
    amax = np.abs(blocks).max(-1, keepdims=True)
    byte = np.maximum(np.where(amax > 0, np.frexp(amax)[1] - 1 + 127, 0) - down, 1)
    scale = np.exp2(byte - 127.0)
    codes = (blocks / scale).astype(np.float32).astype(dtype).astype(np.float64)
    return np.moveaxis((codes * scale).reshape(v.shape), -1, axis)


WIDE = False


def mx_kscale(k):
    if not WIDE:
        return np.ones(k)
    levels = np.array([10, -10, 5, -5, 0])
    if k % 512:
        return np.exp2(np.random.permutation(np.resize(levels, k // 32))).repeat(32)
    a = np.empty((k // 512, 16))
    for p in range(k // 512):
        a[p, :8] = np.random.permutation(np.resize(levels, 8))
        for g in range(8):
            far = levels[np.abs(levels - a[p, g]) >= 10]
            a[p, g + 8] = far[np.random.randint(len(far))]
    return np.exp2(a.ravel()).repeat(32)


def f64(x):
    return np.asarray(x).astype(np.float64)


def striped8(idx):
    return np.concatenate([x.reshape(-1, 16).T for x in idx]).astype(np.uint16)


def runs(offs, k):
    lists = np.stack([offs[16 * r : 16 * r + 16].T.reshape(-1) for r in range(8)]).astype(np.int64)
    return lists[np.arange(k) % 512 // 64]


def pack_weight(w):
    k, n = w.shape
    w = f64(np.asarray(w, np.float32).astype(ml_dtypes.bfloat16)).reshape(k // 32, 32, n)
    amax = np.abs(w).max(1)
    byte = np.clip(np.where(amax > 0, np.frexp(amax)[1] - 1 + 127 - 7, 1), 1, 254)
    scaled = (w * np.exp2(127.0 - byte)[:, None, :]).reshape(k, n).astype(np.float32)
    words = np.ascontiguousarray(scaled.reshape(k // 512, 128, 4, n).transpose(0, 1, 3, 2)).astype(ml_dtypes.float8_e4m3fn).view(np.uint8)
    return words, np.ascontiguousarray(byte.astype(np.uint8).reshape(k // 512, 16, n))


def unpack_weight(words, scales):
    g, p, n, _ = words.shape
    vals = np.ascontiguousarray(words).view(ml_dtypes.float8_e4m3fn).astype(np.float64) * np.repeat(np.exp2(scales.astype(np.float64) - 127.0), 8, axis=1)[..., None]
    return vals.transpose(0, 1, 3, 2).reshape(g * 512, n)


def sigmoid(v):
    return 1.0 / (1.0 + np.exp(-np.maximum(v, -700.0)))


K, T, S, N, H = 512, 2048, 512, 512, 512


def setup_inputs():
    n = np.random.standard_normal
    s = mx_kscale(K)[:, None]
    u = mx_kscale(H)
    packed_xT = pack_weight(n((K, T)) * s)
    return {
        "x_words": packed_xT[0],
        "x_scales": packed_xT[1],
        "w1": (n((K, H)) / np.sqrt(K) / s).astype(np.float32),
        "gn": (np.random.uniform(0.5, 1.5, (H, 1)) * u[:, None]).astype(np.float32),
        "w2": (n((H, N)) / np.sqrt(H) / u[:, None]).astype(np.float32),
        "offs": striped8(np.random.randint(0, T, (8, S))),
        "n1": striped8(np.stack([np.random.permutation(S) for _ in range(8)])),
        "n2": striped8(np.stack([np.random.permutation(S) for _ in range(8)])),
        "n3": striped8(np.stack([np.random.permutation(S) for _ in range(8)])),
        "n4": striped8(np.stack([np.random.permutation(S) for _ in range(8)])),
    }


def reference(x_words, x_scales, w1, gn, w2, offs, n1, n2, n3, n4):
    xq = unpack_weight(x_words, x_scales)[np.arange(K)[:, None], runs(offs, K)]
    y = mxq(f64(w1), 0, "e4m3").T @ xq
    z = f64(gn) * (np.maximum(y * (sigmoid(y[np.arange(H)[:, None], runs(n1, H)])), y[np.arange(H)[:, None], runs(n2, H)]))
    h = mxq(f64(w2), 0, "e4m3").T @ mxq(z, 0, "e4m3")
    return (h[np.arange(N)[:, None], runs(n3, N)]) / (np.abs(h) + np.abs(h[np.arange(N)[:, None], runs(n4, N)]) + 0.5)

@@ -1,0 +1,250 @@
+from contextlib import ExitStack
+
+import concourse.mybir as mybir
+
+F32 = mybir.dt.float32
+BF16 = mybir.dt.bfloat16
+I32 = mybir.dt.int32
+U32 = mybir.dt.uint32
+U16 = mybir.dt.uint16
+U8 = mybir.dt.uint8
+FP8X4 = mybir.dt.float8_e4m3fn_x4
+ALU = mybir.AluOpType
+ACT = mybir.ActivationFunctionType
+
+P = 128
+PACK = 4
+T = 2048
+S = 512
+HALF = S // 2
+LIST_COLS = S // 16
+VECTOR_SHARE = 42
+W2_SHARE = 16
+
+FLOPS = 2 * 2 * 512 * 512 * 512
+
+
+def tile_picked_hashgmaxnorm2_none_p_kernel(tc, x_words, x_scales, w1, gn, w2, offs, n1, n2, n3, n4, out):
+    nc = tc.nc
+    with ExitStack() as ctx:
+        held = ctx.enter_context(tc.tile_pool(name="held", bufs=1))
+        psum = ctx.enter_context(tc.psum_pool(name="psum", bufs=1))
+
+        def load_list(src, name):
+            t = held.tile([P, LIST_COLS], U16, name=name)
+            nc.sync.dma_start(t[:], src)
+            return t
+
+        def half_list(lst, c):
+            return lst[:, c * (LIST_COLS // 2):(c + 1) * (LIST_COLS // 2)]
+
+        scale_table = held.tile([P, T], U8, name="scale_table")
+        nc.vector.memset(scale_table[:].bitcast(I32), 0)
+        warm = held.tile([P, 1], F32, name="warm")
+        warm_out = held.tile([P, 1], F32, name="warm_out")
+        nc.vector.memset(warm[:], 0.0)
+        nc.scalar.activation(warm_out[:], warm[:], ACT.Sigmoid)
+
+        offs_t = load_list(offs, "offs_t")
+        n2_t = load_list(n2, "n2_t")
+        n1_t = load_list(n1, "n1_t")
+        n4_t = load_list(n4, "n4_t")
+        n3_t = load_list(n3, "n3_t")
+        scale_rows = x_scales[0].rearrange("(r e) n -> e r n", e=2)
+        for e in range(2):
+            nc.sync.dma_start(scale_table[:].bitcast(I32)[e:P:16, :], scale_rows[e].bitcast(I32))
+        word_table = held.tile([P, T], I32, name="word_table")
+        nc.sync.dma_start(word_table[:], x_words[0].rearrange("p n t -> p (n t)").bitcast(I32))
+
+        def load_weight(w):
+            rows = w.rearrange("(p j) c -> p j c", j=PACK)
+            parts = []
+            for c in range(2):
+                raw = held.tile([P, PACK, HALF], F32, name="raw", tag="raw%d" % c)
+                nc.sync.dma_start(raw[:], rows[:, :, c * HALF:(c + 1) * HALF])
+                parts.append(raw)
+            return parts
+
+        w1_raw = load_weight(w1)
+        gain = held.tile([P, PACK], F32, name="gain")
+        nc.sync.dma_start(gain[:], gn.rearrange("(p t) o -> p (t o)", t=PACK))
+
+        picked_bytes = held.tile([P, S], U8, name="picked_bytes", align_bytes=64)
+        nc.vector.tensor_copy(picked_bytes[:], scale_table[:].indirect(offs_t[:]))
+        x_plane = held.tile([P, S], U8, name="x_plane", align_bytes=64)
+        nc.vector.tensor_copy(x_plane[:].bitcast(I32), picked_bytes[:].bitcast(I32))
+        for e, queue in ((0, nc.sync), (1, nc.scalar)):
+            queue.dma_start(x_plane[:].bitcast(I32)[2 + e:P:32, :], picked_bytes[:].bitcast(I32)[16 + e:P:32, :])
+        x_codes = held.tile([P, S], U32, name="x_codes", align_bytes=64)
+        nc.vector.tensor_copy(x_codes[:], word_table[:].bitcast(U32).indirect(offs_t[:]))
+
+        gain_abs = held.tile([P, PACK, HALF], F32, name="gain_abs")
+        nc.scalar.activation(gain_abs[:], gain[:].unsqueeze(2).to_broadcast([P, PACK, HALF]), ACT.Abs)
+        gain_sign = held.tile([P, PACK], BF16, name="gain_sign")
+        nc.scalar.activation(gain_sign[:], gain[:], ACT.Sign)
+
+        def deal(grouped, raw, c, lo, hi, engine):
+            dst = grouped[:].rearrange("p (t m j) -> p m t j", t=PACK, j=PACK)[:, 64 * c + lo:64 * c + hi]
+            src = raw[:].rearrange("p j (m t) -> p m t j", t=PACK)[:, lo:hi]
+            if engine is nc.vector:
+                nc.vector.tensor_copy(dst, src)
+            else:
+                nc.scalar.copy(dst, src)
+
+        w1_grouped = held.tile([P, PACK * S], BF16, name="w1_grouped", align_bytes=64)
+        for c in range(2):
+            deal(w1_grouped, w1_raw[c], c, 0, VECTOR_SHARE, nc.vector)
+            deal(w1_grouped, w1_raw[c], c, VECTOR_SHARE, 64, nc.scalar)
+        w1_codes = held.tile([P, S], U32, name="w1_codes", align_bytes=64)
+        w1_plane = held.tile([P, S], U8, name="w1_plane", align_bytes=64)
+        y_bank = []
+        for t in range(PACK):
+            cols = slice(t * P, (t + 1) * P)
+            nc.vector.quantize_mx(out=w1_codes[:, cols].bitcast(FP8X4), scales=w1_plane[:, cols], in_=w1_grouped[:, t * S:(t + 1) * S])
+            bank = psum.tile([P, S], F32, name="y_bank%d" % t, tag="y_bank%d" % t)
+            nc.tensor.matmul_mx(out=bank[:], lhsT=w1_codes[:, cols].bitcast(FP8X4), lhsT_scale=w1_plane[:, cols],
+                                rhs=x_codes[:].bitcast(FP8X4), rhs_scale=x_plane[:], start=True, stop=True)
+            y_bank.append(bank)
+        y = [held.tile([P, S], F32, name="y%d" % t) for t in range(PACK)]
+
+        w2_raw = load_weight(w2)
+
+        gate = [held.tile([P, PACK, HALF], F32, name="gate%d" % c) for c in range(2)]
+        gated = [held.tile([P, PACK, HALF], F32, name="gated%d" % c) for c in range(2)]
+        other = [held.tile([P, PACK, HALF], F32, name="other%d" % c) for c in range(2)]
+        z_mag = held.tile([P, S, PACK], BF16, name="z_mag", align_bytes=64)
+        z_bf = held.tile([P, S, PACK], BF16, name="z_bf", align_bytes=64)
+        z_codes = held.tile([P, S], U32, name="z_codes", align_bytes=64)
+        z_plane = held.tile([P, S], U8, name="z_plane", align_bytes=64)
+
+        def fetch_gate(c, t):
+            nc.scalar.activation(gate[c][:, t, :], y[t][:].indirect(half_list(n1_t, c)), ACT.Sigmoid)
+
+        def fetch_other(c, t):
+            nc.vector.tensor_tensor(other[c][:, t, :], y[t][:].indirect(half_list(n2_t, c)), gain_abs[:, t, :], ALU.mult)
+
+        def apply_gate(c, t):
+            nc.vector.scalar_tensor_tensor(gated[c][:, t, :], y_bank[t][:, c * HALF:(c + 1) * HALF], gain_abs[:, t, 0:1],
+                                           gate[c][:, t, :], ALU.mult, ALU.mult)
+
+        def larger(c, lo, hi):
+            dst = z_mag[:, c * HALF + lo:c * HALF + hi, :].rearrange("p (g i) t -> p g t i", i=4)
+            a = gated[c][:, :, lo:hi].rearrange("p t (g i) -> p g t i", i=4)
+            b = other[c][:, :, lo:hi].rearrange("p t (g i) -> p g t i", i=4)
+            nc.vector.tensor_tensor(dst, a, b, ALU.max)
+
+        def signed(lo, hi):
+            nc.vector.tensor_tensor(z_bf[:, lo:hi, :], z_mag[:, lo:hi, :],
+                                    gain_sign[:].unsqueeze(1).to_broadcast([P, hi - lo, PACK]), ALU.mult)
+
+        def quantise_z(lo, hi):
+            nc.vector.quantize_mx(out=z_codes[:, lo:hi].bitcast(FP8X4), scales=z_plane[:, lo:hi],
+                                  in_=z_bf[:, lo:hi, :].rearrange("p c t -> p (c t)"))
+
+        nc.scalar.copy(y[0][:], y_bank[0][:])
+        nc.vector.tensor_copy(y[1][:], y_bank[1][:])
+        for t in range(PACK):
+            fetch_gate(0, t)
+            if t + 2 < PACK:
+                nc.scalar.copy(y[t + 2][:], y_bank[t + 2][:])
+        for t in range(PACK):
+            fetch_gate(1, t)
+        w2_grouped = held.tile([P, PACK * S], BF16, name="w2_grouped", align_bytes=64)
+        for c in range(2):
+            deal(w2_grouped, w2_raw[c], c, W2_SHARE, 64, nc.scalar)
+        warm2 = held.tile([P, 1], F32, name="warm2")
+        nc.scalar.activation(warm2[:], gate[1][:, PACK - 1, 0:1], ACT.Abs_reciprocal_sqrt, bias=1.0)
+
+        for t in range(PACK):
+            fetch_other(0, t)
+            apply_gate(0, t)
+        fetch_other(1, 0)
+        larger(0, 0, HALF)
+        fetch_other(1, 1)
+        signed(0, HALF)
+        for c in range(2):
+            deal(w2_grouped, w2_raw[c], c, 0, W2_SHARE, nc.vector)
+        quantise_z(0, HALF)
+        fetch_other(1, 2)
+        w2_codes = held.tile([P, S], U32, name="w2_codes", align_bytes=64)
+        w2_plane = held.tile([P, S], U8, name="w2_plane", align_bytes=64)
+        nc.vector.quantize_mx(out=w2_codes[:].bitcast(FP8X4), scales=w2_plane[:], in_=w2_grouped[:])
+        fetch_other(1, 3)
+        for t in range(PACK):
+            apply_gate(1, t)
+        Q = HALF // 2
+        larger(1, 0, Q)
+        larger(1, Q, HALF)
+        signed(HALF, HALF + Q)
+        signed(HALF + Q, S)
+        quantise_z(HALF, HALF + Q)
+        quantise_z(HALF + Q, S)
+
+        h = [held.tile([P, S], F32, name="h%d" % t) for t in range(PACK)]
+        size = [held.tile([P, S], F32, name="size%d" % t) for t in range(PACK)]
+        size_here = [held.tile([P, S], F32, name="size_here%d" % t) for t in range(PACK)]
+        first_banks = [psum.tile([P, 2, HALF], F32, name="first_bank%d" % u) for u in range(2)]
+        quarter_banks = [psum.tile([P, Q], F32, name="quarter_bank%d" % u) for u in range(2)]
+
+        def product(dst, t, lo, hi):
+            cols = slice(t * P, (t + 1) * P)
+            nc.tensor.matmul_mx(out=dst, lhsT=w2_codes[:, cols].bitcast(FP8X4), lhsT_scale=w2_plane[:, cols],
+                                rhs=z_codes[:, lo:hi].bitcast(FP8X4), rhs_scale=z_plane[:, lo:hi], start=True, stop=True)
+
+        first = [first_banks[t % 2][:, t // 2, :] for t in range(PACK)]
+        for t in range(PACK):
+            product(first[t], t, 0, HALF)
+        for t in range(PACK):
+            nc.scalar.activation(size[t][:, :HALF], first[t], ACT.Abs)
+        for t in range(PACK):
+            nc.scalar.copy(h[t][:, :HALF], first[t])
+        for t in range(PACK):
+            nc.vector.tensor_copy(size_here[t][:, :HALF], size[t][:, :HALF])
+        second = [None]
+        for u in range(2):
+            product(quarter_banks[u][:], 0, HALF + u * Q, HALF + (u + 1) * Q)
+        for t in range(1, PACK):
+            bank = psum.tile([P, HALF], F32, name="second_bank%d" % t, tag="y_bank%d" % (t - 1))
+            product(bank[:], t, HALF, S)
+            second.append(bank)
+
+        def empty(t):
+            if t == 0:
+                pieces = [(quarter_banks[u][:], slice(HALF + u * Q, HALF + (u + 1) * Q)) for u in range(2)]
+            else:
+                pieces = [(second[t][:], slice(HALF, S))]
+            for src, cols in pieces:
+                nc.scalar.activation(size[t][:, cols], src, ACT.Abs)
+            for src, cols in pieces:
+                nc.scalar.activation(size_here[t][:, cols], src, ACT.Abs)
+            for src, cols in pieces:
+                nc.scalar.copy(h[t][:, cols], src)
+
+        total = [held.tile([P, S], F32, name="total%d" % t) for t in range(PACK)]
+        root = [held.tile([P, S], F32, name="root%d" % t) for t in range(PACK)]
+        inverse = [held.tile([P, S], F32, name="inverse%d" % t) for t in range(PACK)]
+        result = [held.tile([P, S], F32, name="result%d" % t) for t in range(PACK)]
+        out_rows = out.rearrange("(p t) c -> p t c", t=PACK)
+
+        def denominator(t, c):
+            half = slice(c * HALF, (c + 1) * HALF)
+            nc.vector.tensor_tensor(total[t][:, half], size[t][:].indirect(half_list(n4_t, c)), size_here[t][:, half], ALU.add)
+            nc.scalar.activation(root[t][:, half], total[t][:, half], ACT.Abs_reciprocal_sqrt, bias=0.5)
+            nc.scalar.activation(inverse[t][:, half], root[t][:, half], ACT.Square)
+
+        def finish(t, c):
+            half = slice(c * HALF, (c + 1) * HALF)
+            nc.vector.tensor_tensor(result[t][:, half], h[t][:].indirect(half_list(n3_t, c)), inverse[t][:, half], ALU.mult)
+            nc.sync.dma_start(out_rows[:, t, half], result[t][:, half])
+
+        empty(0)
+        for t in range(PACK):
+            if t + 1 < PACK:
+                empty(t + 1)
+            denominator(t, 0)
+            denominator(t, 1)
+            if t > 0:
+                finish(t - 1, 0)
+                finish(t - 1, 1)
+        finish(PACK - 1, 0)
+        finish(PACK - 1, 1)

@@ -19,7 +19,6 @@ S = 512
 HALF = S // 2
 LIST_COLS = S // 16
 VECTOR_SHARE = 42
-W2_SHARE = 16
 
 FLOPS = 2 * 2 * 512 * 512 * 512
 
@@ -34,9 +33,6 @@ def tile_picked_hashgmaxnorm2_none_p_kernel(tc, x_words, x_scales, w1, gn, w2, o
             t = held.tile([P, LIST_COLS], U16, name=name)
             nc.sync.dma_start(t[:], src)
             return t
-
-        def half_list(lst, c):
-            return lst[:, c * (LIST_COLS // 2):(c + 1) * (LIST_COLS // 2)]
 
         scale_table = held.tile([P, T], U8, name="scale_table")
         nc.vector.memset(scale_table[:].bitcast(I32), 0)
@@ -53,39 +49,46 @@ def tile_picked_hashgmaxnorm2_none_p_kernel(tc, x_words, x_scales, w1, gn, w2, o
         scale_rows = x_scales[0].rearrange("(r e) n -> e r n", e=2)
         for e in range(2):
             nc.sync.dma_start(scale_table[:].bitcast(I32)[e:P:16, :], scale_rows[e].bitcast(I32))
-        word_table = held.tile([P, T], I32, name="word_table")
+        word_table = held.tile([P, T], I32, name="word_table", tag="word_table")
         nc.sync.dma_start(word_table[:], x_words[0].rearrange("p n t -> p (n t)").bitcast(I32))
 
-        def load_weight(w):
-            rows = w.rearrange("(p j) c -> p j c", j=PACK)
-            parts = []
-            for c in range(2):
-                raw = held.tile([P, PACK, HALF], F32, name="raw", tag="raw%d" % c)
-                nc.sync.dma_start(raw[:], rows[:, :, c * HALF:(c + 1) * HALF])
-                parts.append(raw)
-            return parts
-
-        w1_raw = load_weight(w1)
         gain = held.tile([P, PACK], F32, name="gain")
         nc.sync.dma_start(gain[:], gn.rearrange("(p t) o -> p (t o)", t=PACK))
+        w1_rows = w1.rearrange("(p j) c -> p j c", j=PACK)
+        w1_raw = []
+        for c in range(2):
+            raw = held.tile([P, PACK, HALF], F32, name="w1_raw%d" % c)
+            nc.sync.dma_start(raw[:], w1_rows[:, :, c * HALF:(c + 1) * HALF])
+            w1_raw.append(raw)
 
         picked_bytes = held.tile([P, S], U8, name="picked_bytes", align_bytes=64)
         nc.vector.tensor_copy(picked_bytes[:], scale_table[:].indirect(offs_t[:]))
         x_plane = held.tile([P, S], U8, name="x_plane", align_bytes=64)
         nc.vector.tensor_copy(x_plane[:].bitcast(I32), picked_bytes[:].bitcast(I32))
-        for e, queue in ((0, nc.sync), (1, nc.scalar)):
-            queue.dma_start(x_plane[:].bitcast(I32)[2 + e:P:32, :], picked_bytes[:].bitcast(I32)[16 + e:P:32, :])
+        for e in range(2):
+            nc.scalar.dma_start(x_plane[:].bitcast(I32)[2 + e:P:32, :], picked_bytes[:].bitcast(I32)[16 + e:P:32, :])
         x_codes = held.tile([P, S], U32, name="x_codes", align_bytes=64)
         nc.vector.tensor_copy(x_codes[:], word_table[:].bitcast(U32).indirect(offs_t[:]))
+        w2_raw = held.tile([P, PACK, S], F32, name="w2_raw", tag="word_table")
+        nc.sync.dma_start(w2_raw[:], w2.rearrange("(p j) c -> p j c", j=PACK))
 
-        gain_abs = held.tile([P, PACK, HALF], F32, name="gain_abs")
-        nc.scalar.activation(gain_abs[:], gain[:].unsqueeze(2).to_broadcast([P, PACK, HALF]), ACT.Abs)
+        y_window = [held.tile([P, 2 * S], F32, name="y_window%d" % t) for t in range(PACK)]
+        size_window = [held.tile([P, 2 * S], F32, name="size_window%d" % t) for t in range(PACK)]
+        h_window = [held.tile([P, 2 * S], F32, name="h_window%d" % t) for t in range(PACK)]
+        y = [y_window[t][:, :S] for t in range(PACK)]
+        gain_abs = [y_window[(t + 1) % PACK][:, S:] for t in range(PACK)]
+        size = [size_window[t][:, :S] for t in range(PACK)]
+        gate = [size_window[t][:, S:] for t in range(PACK)]
+        h = [h_window[t][:, :S] for t in range(PACK)]
+        size_here = [h_window[t][:, S:] for t in range(PACK)]
+        for t in range(PACK):
+            nc.scalar.activation(gain_abs[t], gain[:, t:t + 1].to_broadcast([P, S]), ACT.Abs)
         gain_sign = held.tile([P, PACK], BF16, name="gain_sign")
         nc.scalar.activation(gain_sign[:], gain[:], ACT.Sign)
 
         def deal(grouped, raw, c, lo, hi, engine):
-            dst = grouped[:].rearrange("p (t m j) -> p m t j", t=PACK, j=PACK)[:, 64 * c + lo:64 * c + hi]
-            src = raw[:].rearrange("p j (m t) -> p m t j", t=PACK)[:, lo:hi]
+            dst = grouped[:].rearrange("p (t m j) -> p m j t", t=PACK, j=PACK)[:, 64 * c + lo:64 * c + hi]
+            src = raw[:].rearrange("p j (m t) -> p m j t", t=PACK)[:, lo:hi]
             if engine is nc.vector:
                 nc.vector.tensor_copy(dst, src)
             else:
@@ -97,40 +100,41 @@ def tile_picked_hashgmaxnorm2_none_p_kernel(tc, x_words, x_scales, w1, gn, w2, o
             deal(w1_grouped, w1_raw[c], c, VECTOR_SHARE, 64, nc.scalar)
         w1_codes = held.tile([P, S], U32, name="w1_codes", align_bytes=64)
         w1_plane = held.tile([P, S], U8, name="w1_plane", align_bytes=64)
-        y_bank = []
+        y_sums = []
         for t in range(PACK):
             cols = slice(t * P, (t + 1) * P)
             nc.vector.quantize_mx(out=w1_codes[:, cols].bitcast(FP8X4), scales=w1_plane[:, cols], in_=w1_grouped[:, t * S:(t + 1) * S])
-            bank = psum.tile([P, S], F32, name="y_bank%d" % t, tag="y_bank%d" % t)
-            nc.tensor.matmul_mx(out=bank[:], lhsT=w1_codes[:, cols].bitcast(FP8X4), lhsT_scale=w1_plane[:, cols],
-                                rhs=x_codes[:].bitcast(FP8X4), rhs_scale=x_plane[:], start=True, stop=True)
-            y_bank.append(bank)
-        y = [held.tile([P, S], F32, name="y%d" % t) for t in range(PACK)]
+            pieces = []
+            for u, places in enumerate([slice(0, HALF), slice(HALF, S)] if t == 0 else [slice(0, S)]):
+                bank = psum.tile([P, places.stop - places.start], F32, name="y_bank", tag="bank%d_%d" % (t, u))
+                nc.tensor.matmul_mx(out=bank[:], lhsT=w1_codes[:, cols].bitcast(FP8X4), lhsT_scale=w1_plane[:, cols],
+                                    rhs=x_codes[:, places].bitcast(FP8X4), rhs_scale=x_plane[:, places], start=True, stop=True)
+                pieces.append((bank, places))
+            y_sums.append(pieces)
 
-        w2_raw = load_weight(w2)
-
-        gate = [held.tile([P, PACK, HALF], F32, name="gate%d" % c) for c in range(2)]
         gated = [held.tile([P, PACK, HALF], F32, name="gated%d" % c) for c in range(2)]
-        other = [held.tile([P, PACK, HALF], F32, name="other%d" % c) for c in range(2)]
+        other = held.tile([P, PACK, S], F32, name="other")
         z_mag = held.tile([P, S, PACK], BF16, name="z_mag", align_bytes=64)
         z_bf = held.tile([P, S, PACK], BF16, name="z_bf", align_bytes=64)
         z_codes = held.tile([P, S], U32, name="z_codes", align_bytes=64)
         z_plane = held.tile([P, S], U8, name="z_plane", align_bytes=64)
 
-        def fetch_gate(c, t):
-            nc.scalar.activation(gate[c][:, t, :], y[t][:].indirect(half_list(n1_t, c)), ACT.Sigmoid)
+        def fetch_gate(t, c):
+            lo, hi = c * HALF, (c + 1) * HALF
+            nc.scalar.activation(gate[t][:, lo:hi], y_window[t][:].indirect(n1_t[:, lo // 16:hi // 16]), ACT.Sigmoid)
 
-        def fetch_other(c, t):
-            nc.vector.tensor_tensor(other[c][:, t, :], y[t][:].indirect(half_list(n2_t, c)), gain_abs[:, t, :], ALU.mult)
+        def fetch_other(t):
+            nc.vector.tensor_tensor(other[:, t, :], y_window[t][:].indirect(n2_t[:]), gain_abs[t], ALU.mult)
 
-        def apply_gate(c, t):
-            nc.vector.scalar_tensor_tensor(gated[c][:, t, :], y_bank[t][:, c * HALF:(c + 1) * HALF], gain_abs[:, t, 0:1],
-                                           gate[c][:, t, :], ALU.mult, ALU.mult)
+        def apply_gate(t, c):
+            places = slice(c * HALF, (c + 1) * HALF)
+            sums = y_sums[0][c][0][:] if t == 0 else y_sums[t][0][0][:, places]
+            nc.vector.scalar_tensor_tensor(gated[c][:, t, :], sums, gain_abs[t][:, 0:1], gate[t][:, places], ALU.mult, ALU.mult)
 
-        def larger(c, lo, hi):
-            dst = z_mag[:, c * HALF + lo:c * HALF + hi, :].rearrange("p (g i) t -> p g t i", i=4)
-            a = gated[c][:, :, lo:hi].rearrange("p t (g i) -> p g t i", i=4)
-            b = other[c][:, :, lo:hi].rearrange("p t (g i) -> p g t i", i=4)
+        def larger(lo, hi):
+            dst = z_mag[:, lo:hi, :].rearrange("p (g i) t -> p g t i", i=4)
+            a = gated[lo // HALF][:, :, lo % HALF:lo % HALF + hi - lo].rearrange("p t (g i) -> p g t i", i=4)
+            b = other[:, :, lo:hi].rearrange("p t (g i) -> p g t i", i=4)
             nc.vector.tensor_tensor(dst, a, b, ALU.max)
 
         def signed(lo, hi):
@@ -141,50 +145,43 @@ def tile_picked_hashgmaxnorm2_none_p_kernel(tc, x_words, x_scales, w1, gn, w2, o
             nc.vector.quantize_mx(out=z_codes[:, lo:hi].bitcast(FP8X4), scales=z_plane[:, lo:hi],
                                   in_=z_bf[:, lo:hi, :].rearrange("p c t -> p (c t)"))
 
-        nc.scalar.copy(y[0][:], y_bank[0][:])
-        nc.vector.tensor_copy(y[1][:], y_bank[1][:])
+        nc.scalar.copy(y[0][:, :HALF], y_sums[0][0][0][:])
+        nc.vector.tensor_copy(y[0][:, HALF:], y_sums[0][1][0][:])
         for t in range(PACK):
-            fetch_gate(0, t)
-            if t + 2 < PACK:
-                nc.scalar.copy(y[t + 2][:], y_bank[t + 2][:])
-        for t in range(PACK):
-            fetch_gate(1, t)
+            if t + 1 < PACK:
+                nc.scalar.copy(y[t + 1], y_sums[t + 1][0][0][:])
+            fetch_gate(t, 0)
         w2_grouped = held.tile([P, PACK * S], BF16, name="w2_grouped", align_bytes=64)
-        for c in range(2):
-            deal(w2_grouped, w2_raw[c], c, W2_SHARE, 64, nc.scalar)
-        warm2 = held.tile([P, 1], F32, name="warm2")
-        nc.scalar.activation(warm2[:], gate[1][:, PACK - 1, 0:1], ACT.Abs_reciprocal_sqrt, bias=1.0)
-
+        deal(w2_grouped, w2_raw, 0, 0, P, nc.scalar)
         for t in range(PACK):
-            fetch_other(0, t)
-            apply_gate(0, t)
-        fetch_other(1, 0)
-        larger(0, 0, HALF)
-        fetch_other(1, 1)
-        signed(0, HALF)
-        for c in range(2):
-            deal(w2_grouped, w2_raw[c], c, 0, W2_SHARE, nc.vector)
-        quantise_z(0, HALF)
-        fetch_other(1, 2)
+            fetch_gate(t, 1)
+        warm2 = held.tile([P, 1], F32, name="warm2")
+        nc.scalar.activation(warm2[:], gate[PACK - 1][:, S - 1:], ACT.Abs_reciprocal_sqrt, bias=1.0)
+
+        fetch_other(0)
+        for t in range(PACK):
+            if t + 1 < PACK:
+                fetch_other(t + 1)
+            apply_gate(t, 0)
+        Q = HALF // 2
         w2_codes = held.tile([P, S], U32, name="w2_codes", align_bytes=64)
         w2_plane = held.tile([P, S], U8, name="w2_plane", align_bytes=64)
+        larger(0, HALF)
         nc.vector.quantize_mx(out=w2_codes[:].bitcast(FP8X4), scales=w2_plane[:], in_=w2_grouped[:])
-        fetch_other(1, 3)
-        for t in range(PACK):
-            apply_gate(1, t)
-        Q = HALF // 2
-        larger(1, 0, Q)
-        larger(1, Q, HALF)
+        signed(0, HALF)
+        apply_gate(0, 1)
+        quantise_z(0, HALF)
+        for t in range(1, PACK):
+            apply_gate(t, 1)
+        larger(HALF, HALF + Q)
+        larger(HALF + Q, S)
         signed(HALF, HALF + Q)
         signed(HALF + Q, S)
         quantise_z(HALF, HALF + Q)
         quantise_z(HALF + Q, S)
 
-        h = [held.tile([P, S], F32, name="h%d" % t) for t in range(PACK)]
-        size = [held.tile([P, S], F32, name="size%d" % t) for t in range(PACK)]
-        size_here = [held.tile([P, S], F32, name="size_here%d" % t) for t in range(PACK)]
         first_banks = [psum.tile([P, 2, HALF], F32, name="first_bank%d" % u) for u in range(2)]
-        quarter_banks = [psum.tile([P, Q], F32, name="quarter_bank%d" % u) for u in range(2)]
+        quarter_banks = [psum.tile([P, Q], F32, name="quarter_bank", tag="bank0_%d" % u) for u in range(2)]
 
         def product(dst, t, lo, hi):
             cols = slice(t * P, (t + 1) * P)
@@ -204,21 +201,19 @@ def tile_picked_hashgmaxnorm2_none_p_kernel(tc, x_words, x_scales, w1, gn, w2, o
         for u in range(2):
             product(quarter_banks[u][:], 0, HALF + u * Q, HALF + (u + 1) * Q)
         for t in range(1, PACK):
-            bank = psum.tile([P, HALF], F32, name="second_bank%d" % t, tag="y_bank%d" % (t - 1))
+            bank = psum.tile([P, HALF], F32, name="second_bank", tag="bank%d_0" % t)
             product(bank[:], t, HALF, S)
             second.append(bank)
 
-        def empty(t):
+        def second_pieces(t):
             if t == 0:
-                pieces = [(quarter_banks[u][:], slice(HALF + u * Q, HALF + (u + 1) * Q)) for u in range(2)]
-            else:
-                pieces = [(second[t][:], slice(HALF, S))]
-            for src, cols in pieces:
-                nc.scalar.activation(size[t][:, cols], src, ACT.Abs)
-            for src, cols in pieces:
-                nc.scalar.activation(size_here[t][:, cols], src, ACT.Abs)
-            for src, cols in pieces:
-                nc.scalar.copy(h[t][:, cols], src)
+                return [(quarter_banks[u][:], slice(HALF + u * Q, HALF + (u + 1) * Q)) for u in range(2)]
+            return [(second[t][:], slice(HALF, S))]
+
+        def sizes(t):
+            for dst in (size, size_here):
+                for src, cols in second_pieces(t):
+                    nc.scalar.activation(dst[t][:, cols], src, ACT.Abs)
 
         total = [held.tile([P, S], F32, name="total%d" % t) for t in range(PACK)]
         root = [held.tile([P, S], F32, name="root%d" % t) for t in range(PACK)]
@@ -226,25 +221,35 @@ def tile_picked_hashgmaxnorm2_none_p_kernel(tc, x_words, x_scales, w1, gn, w2, o
         result = [held.tile([P, S], F32, name="result%d" % t) for t in range(PACK)]
         out_rows = out.rearrange("(p t) c -> p t c", t=PACK)
 
-        def denominator(t, c):
-            half = slice(c * HALF, (c + 1) * HALF)
-            nc.vector.tensor_tensor(total[t][:, half], size[t][:].indirect(half_list(n4_t, c)), size_here[t][:, half], ALU.add)
-            nc.scalar.activation(root[t][:, half], total[t][:, half], ACT.Abs_reciprocal_sqrt, bias=0.5)
-            nc.scalar.activation(inverse[t][:, half], root[t][:, half], ACT.Square)
+        def add_sizes(t):
+            cuts = [0, HALF, S] if t == 0 else [0, S]
+            for lo, hi in zip(cuts, cuts[1:]):
+                nc.vector.tensor_tensor(total[t][:, lo:hi], size_window[t][:].indirect(n4_t[:, lo // 16:hi // 16]), size_here[t][:, lo:hi], ALU.add)
 
-        def finish(t, c):
-            half = slice(c * HALF, (c + 1) * HALF)
-            nc.vector.tensor_tensor(result[t][:, half], h[t][:].indirect(half_list(n3_t, c)), inverse[t][:, half], ALU.mult)
-            nc.sync.dma_start(out_rows[:, t, half], result[t][:, half])
+        def last_cuts(t):
+            cuts = [0, S - Q, S] if t == PACK - 1 else [0, S]
+            return list(zip(cuts, cuts[1:]))
 
-        empty(0)
-        for t in range(PACK):
-            if t + 1 < PACK:
-                empty(t + 1)
-            denominator(t, 0)
-            denominator(t, 1)
-            if t > 0:
-                finish(t - 1, 0)
-                finish(t - 1, 1)
-        finish(PACK - 1, 0)
-        finish(PACK - 1, 1)
+        def invert(t):
+            for lo, hi in last_cuts(t):
+                nc.scalar.activation(root[t][:, lo:hi], total[t][:, lo:hi], ACT.Abs_reciprocal_sqrt, bias=0.5)
+            for src, cols in second_pieces(t):
+                nc.scalar.copy(h[t][:, cols], src)
+            for lo, hi in last_cuts(t):
+                nc.scalar.activation(inverse[t][:, lo:hi], root[t][:, lo:hi], ACT.Square)
+
+        def finish(t):
+            for lo, hi in last_cuts(t):
+                nc.vector.tensor_tensor(result[t][:, lo:hi], h_window[t][:].indirect(n3_t[:, lo // 16:hi // 16]), inverse[t][:, lo:hi], ALU.mult)
+                nc.sync.dma_start(out_rows[:, t, lo:hi], result[t][:, lo:hi])
+
+        for t in range(PACK - 1):
+            sizes(t)
+            add_sizes(t)
+        invert(0)
+        finish(0)
+        sizes(PACK - 1)
+        add_sizes(PACK - 1)
+        for t in range(1, PACK):
+            invert(t)
+            finish(t)

@@ -42,31 +42,31 @@ def tile_picked_hashgmaxnorm2_none_p_kernel(tc, x_words, x_scales, w1, gn, w2, o
         nc.scalar.activation(warm_out[:], warm[:], ACT.Sigmoid)
 
         offs_t = load_list(offs, "offs_t")
+        gain = held.tile([P, PACK], F32, name="gain")
+        nc.sync.dma_start(gain[:], gn.rearrange("(p t) o -> p (t o)", t=PACK))
         n2_t = load_list(n2, "n2_t")
         n1_t = load_list(n1, "n1_t")
-        n4_t = load_list(n4, "n4_t")
-        n3_t = load_list(n3, "n3_t")
         scale_rows = x_scales[0].rearrange("(r e) n -> e r n", e=2)
         for e in range(2):
             nc.sync.dma_start(scale_table[:].bitcast(I32)[e:P:16, :], scale_rows[e].bitcast(I32))
         word_table = held.tile([P, T], I32, name="word_table", tag="word_table")
         nc.sync.dma_start(word_table[:], x_words[0].rearrange("p n t -> p (n t)").bitcast(I32))
 
-        gain = held.tile([P, PACK], F32, name="gain")
-        nc.sync.dma_start(gain[:], gn.rearrange("(p t) o -> p (t o)", t=PACK))
         w1_rows = w1.rearrange("(p j) c -> p j c", j=PACK)
         w1_raw = []
         for c in range(2):
             raw = held.tile([P, PACK, HALF], F32, name="w1_raw%d" % c)
             nc.sync.dma_start(raw[:], w1_rows[:, :, c * HALF:(c + 1) * HALF])
             w1_raw.append(raw)
+        n4_t = load_list(n4, "n4_t")
+        n3_t = load_list(n3, "n3_t")
 
         picked_bytes = held.tile([P, S], U8, name="picked_bytes", align_bytes=64)
         nc.vector.tensor_copy(picked_bytes[:], scale_table[:].indirect(offs_t[:]))
         x_plane = held.tile([P, S], U8, name="x_plane", align_bytes=64)
         nc.vector.tensor_copy(x_plane[:].bitcast(I32), picked_bytes[:].bitcast(I32))
         for e in range(2):
-            nc.scalar.dma_start(x_plane[:].bitcast(I32)[2 + e:P:32, :], picked_bytes[:].bitcast(I32)[16 + e:P:32, :])
+            nc.sync.dma_start(x_plane[:].bitcast(I32)[2 + e:P:32, :], picked_bytes[:].bitcast(I32)[16 + e:P:32, :])
         x_codes = held.tile([P, S], U32, name="x_codes", align_bytes=64)
         nc.vector.tensor_copy(x_codes[:], word_table[:].bitcast(U32).indirect(offs_t[:]))
         w2_raw = held.tile([P, PACK, S], F32, name="w2_raw", tag="word_table")
@@ -132,9 +132,9 @@ def tile_picked_hashgmaxnorm2_none_p_kernel(tc, x_words, x_scales, w1, gn, w2, o
             nc.vector.scalar_tensor_tensor(gated[c][:, t, :], sums, gain_abs[t][:, 0:1], gate[t][:, places], ALU.mult, ALU.mult)
 
         def larger(lo, hi):
-            dst = z_mag[:, lo:hi, :].rearrange("p (g i) t -> p g t i", i=4)
-            a = gated[lo // HALF][:, :, lo % HALF:lo % HALF + hi - lo].rearrange("p t (g i) -> p g t i", i=4)
-            b = other[:, :, lo:hi].rearrange("p t (g i) -> p g t i", i=4)
+            dst = z_mag[:, lo:hi, :].rearrange("p (g i) t -> p g t i", i=2)
+            a = gated[lo // HALF][:, :, lo % HALF:lo % HALF + hi - lo].rearrange("p t (g i) -> p g t i", i=2)
+            b = other[:, :, lo:hi].rearrange("p t (g i) -> p g t i", i=2)
             nc.vector.tensor_tensor(dst, a, b, ALU.max)
 
         def signed(lo, hi):
@@ -241,7 +241,7 @@ def tile_picked_hashgmaxnorm2_none_p_kernel(tc, x_words, x_scales, w1, gn, w2, o
         def finish(t):
             for lo, hi in last_cuts(t):
                 nc.vector.tensor_tensor(result[t][:, lo:hi], h_window[t][:].indirect(n3_t[:, lo // 16:hi // 16]), inverse[t][:, lo:hi], ALU.mult)
-                nc.sync.dma_start(out_rows[:, t, lo:hi], result[t][:, lo:hi])
+                (nc.scalar if lo > 0 else nc.sync).dma_start(out_rows[:, t, lo:hi], result[t][:, lo:hi])
 
         for t in range(PACK - 1):
             sizes(t)

from contextlib import ExitStack

import concourse.mybir as mybir

F32 = mybir.dt.float32
BF16 = mybir.dt.bfloat16
I32 = mybir.dt.int32
U32 = mybir.dt.uint32
U16 = mybir.dt.uint16
U8 = mybir.dt.uint8
FP8X4 = mybir.dt.float8_e4m3fn_x4
ALU = mybir.AluOpType
ACT = mybir.ActivationFunctionType

P = 128
PACK = 4
T = 2048
S = 512
HALF = S // 2
LIST_COLS = S // 16
VECTOR_SHARE = 42

FLOPS = 2 * 2 * 512 * 512 * 512


def tile_picked_hashgmaxnorm2_none_p_kernel(tc, x_words, x_scales, w1, gn, w2, offs, n1, n2, n3, n4, out):
    nc = tc.nc
    with ExitStack() as ctx:
        held = ctx.enter_context(tc.tile_pool(name="held", bufs=1))
        psum = ctx.enter_context(tc.psum_pool(name="psum", bufs=1))

        def load_list(src, name):
            t = held.tile([P, LIST_COLS], U16, name=name)
            nc.sync.dma_start(t[:], src)
            return t

        scale_table = held.tile([P, T], U8, name="scale_table")
        nc.vector.memset(scale_table[:].bitcast(I32), 0)
        warm = held.tile([P, 1], F32, name="warm")
        warm_out = held.tile([P, 1], F32, name="warm_out")
        nc.vector.memset(warm[:], 0.0)
        nc.scalar.activation(warm_out[:], warm[:], ACT.Sigmoid)

        offs_t = load_list(offs, "offs_t")
        gain = held.tile([P, PACK], F32, name="gain")
        nc.sync.dma_start(gain[:], gn.rearrange("(p t) o -> p (t o)", t=PACK))
        n2_t = load_list(n2, "n2_t")
        n1_t = load_list(n1, "n1_t")
        scale_rows = x_scales[0].rearrange("(r e) n -> e r n", e=2)
        for e in range(2):
            nc.sync.dma_start(scale_table[:].bitcast(I32)[e:P:16, :], scale_rows[e].bitcast(I32))
        word_table = held.tile([P, T], I32, name="word_table", tag="word_table")
        nc.sync.dma_start(word_table[:], x_words[0].rearrange("p n t -> p (n t)").bitcast(I32))

        w1_rows = w1.rearrange("(p j) c -> p j c", j=PACK)
        w1_raw = []
        for c in range(2):
            raw = held.tile([P, PACK, HALF], F32, name="w1_raw%d" % c)
            nc.sync.dma_start(raw[:], w1_rows[:, :, c * HALF:(c + 1) * HALF])
            w1_raw.append(raw)
        n4_t = load_list(n4, "n4_t")
        n3_t = load_list(n3, "n3_t")

        picked_bytes = held.tile([P, S], U8, name="picked_bytes", align_bytes=64)
        nc.vector.tensor_copy(picked_bytes[:], scale_table[:].indirect(offs_t[:]))
        x_plane = held.tile([P, S], U8, name="x_plane", align_bytes=64)
        nc.vector.tensor_copy(x_plane[:].bitcast(I32), picked_bytes[:].bitcast(I32))
        for e in range(2):
            nc.sync.dma_start(x_plane[:].bitcast(I32)[2 + e:P:32, :], picked_bytes[:].bitcast(I32)[16 + e:P:32, :])
        x_codes = held.tile([P, S], U32, name="x_codes", align_bytes=64)
        nc.vector.tensor_copy(x_codes[:], word_table[:].bitcast(U32).indirect(offs_t[:]))
        w2_raw = held.tile([P, PACK, S], F32, name="w2_raw", tag="word_table")
        nc.sync.dma_start(w2_raw[:], w2.rearrange("(p j) c -> p j c", j=PACK))

        y_window = [held.tile([P, 2 * S], F32, name="y_window%d" % t) for t in range(PACK)]
        size_window = [held.tile([P, 2 * S], F32, name="size_window%d" % t) for t in range(PACK)]
        h_window = [held.tile([P, 2 * S], F32, name="h_window%d" % t) for t in range(PACK)]
        y = [y_window[t][:, :S] for t in range(PACK)]
        gain_abs = [y_window[(t + 1) % PACK][:, S:] for t in range(PACK)]
        size = [size_window[t][:, :S] for t in range(PACK)]
        gate = [size_window[t][:, S:] for t in range(PACK)]
        h = [h_window[t][:, :S] for t in range(PACK)]
        size_here = [h_window[t][:, S:] for t in range(PACK)]
        for t in range(PACK):
            nc.scalar.activation(gain_abs[t], gain[:, t:t + 1].to_broadcast([P, S]), ACT.Abs)
        gain_sign = held.tile([P, PACK], BF16, name="gain_sign")
        nc.scalar.activation(gain_sign[:], gain[:], ACT.Sign)

        def deal(grouped, raw, c, lo, hi, engine):
            dst = grouped[:].rearrange("p (t m j) -> p m j t", t=PACK, j=PACK)[:, 64 * c + lo:64 * c + hi]
            src = raw[:].rearrange("p j (m t) -> p m j t", t=PACK)[:, lo:hi]
            if engine is nc.vector:
                nc.vector.tensor_copy(dst, src)
            else:
                nc.scalar.copy(dst, src)

        w1_grouped = held.tile([P, PACK * S], BF16, name="w1_grouped", align_bytes=64)
        for c in range(2):
            deal(w1_grouped, w1_raw[c], c, 0, VECTOR_SHARE, nc.vector)
            deal(w1_grouped, w1_raw[c], c, VECTOR_SHARE, 64, nc.scalar)
        w1_codes = held.tile([P, S], U32, name="w1_codes", align_bytes=64)
        w1_plane = held.tile([P, S], U8, name="w1_plane", align_bytes=64)
        y_sums = []
        for t in range(PACK):
            cols = slice(t * P, (t + 1) * P)
            nc.vector.quantize_mx(out=w1_codes[:, cols].bitcast(FP8X4), scales=w1_plane[:, cols], in_=w1_grouped[:, t * S:(t + 1) * S])
            pieces = []
            for u, places in enumerate([slice(0, HALF), slice(HALF, S)] if t == 0 else [slice(0, S)]):
                bank = psum.tile([P, places.stop - places.start], F32, name="y_bank", tag="bank%d_%d" % (t, u))
                nc.tensor.matmul_mx(out=bank[:], lhsT=w1_codes[:, cols].bitcast(FP8X4), lhsT_scale=w1_plane[:, cols],
                                    rhs=x_codes[:, places].bitcast(FP8X4), rhs_scale=x_plane[:, places], start=True, stop=True)
                pieces.append((bank, places))
            y_sums.append(pieces)

        gated = [held.tile([P, PACK, HALF], F32, name="gated%d" % c) for c in range(2)]
        other = held.tile([P, PACK, S], F32, name="other")
        z_mag = held.tile([P, S, PACK], BF16, name="z_mag", align_bytes=64)
        z_bf = held.tile([P, S, PACK], BF16, name="z_bf", align_bytes=64)
        z_codes = held.tile([P, S], U32, name="z_codes", align_bytes=64)
        z_plane = held.tile([P, S], U8, name="z_plane", align_bytes=64)

        def fetch_gate(t, c):
            lo, hi = c * HALF, (c + 1) * HALF
            nc.scalar.activation(gate[t][:, lo:hi], y_window[t][:].indirect(n1_t[:, lo // 16:hi // 16]), ACT.Sigmoid)

        def fetch_other(t):
            nc.vector.tensor_tensor(other[:, t, :], y_window[t][:].indirect(n2_t[:]), gain_abs[t], ALU.mult)

        def apply_gate(t, c):
            places = slice(c * HALF, (c + 1) * HALF)
            sums = y_sums[0][c][0][:] if t == 0 else y_sums[t][0][0][:, places]
            nc.vector.scalar_tensor_tensor(gated[c][:, t, :], sums, gain_abs[t][:, 0:1], gate[t][:, places], ALU.mult, ALU.mult)

        def larger(lo, hi):
            dst = z_mag[:, lo:hi, :].rearrange("p (g i) t -> p g t i", i=2)
            a = gated[lo // HALF][:, :, lo % HALF:lo % HALF + hi - lo].rearrange("p t (g i) -> p g t i", i=2)
            b = other[:, :, lo:hi].rearrange("p t (g i) -> p g t i", i=2)
            nc.vector.tensor_tensor(dst, a, b, ALU.max)

        def signed(lo, hi):
            nc.vector.tensor_tensor(z_bf[:, lo:hi, :], z_mag[:, lo:hi, :],
                                    gain_sign[:].unsqueeze(1).to_broadcast([P, hi - lo, PACK]), ALU.mult)

        def quantise_z(lo, hi):
            nc.vector.quantize_mx(out=z_codes[:, lo:hi].bitcast(FP8X4), scales=z_plane[:, lo:hi],
                                  in_=z_bf[:, lo:hi, :].rearrange("p c t -> p (c t)"))

        nc.scalar.copy(y[0][:, :HALF], y_sums[0][0][0][:])
        nc.vector.tensor_copy(y[0][:, HALF:], y_sums[0][1][0][:])
        for t in range(PACK):
            if t + 1 < PACK:
                nc.scalar.copy(y[t + 1], y_sums[t + 1][0][0][:])
            fetch_gate(t, 0)
        w2_grouped = held.tile([P, PACK * S], BF16, name="w2_grouped", align_bytes=64)
        deal(w2_grouped, w2_raw, 0, 0, P, nc.scalar)
        for t in range(PACK):
            fetch_gate(t, 1)
        warm2 = held.tile([P, 1], F32, name="warm2")
        nc.scalar.activation(warm2[:], gate[PACK - 1][:, S - 1:], ACT.Abs_reciprocal_sqrt, bias=1.0)

        fetch_other(0)
        for t in range(PACK):
            if t + 1 < PACK:
                fetch_other(t + 1)
            apply_gate(t, 0)
        Q = HALF // 2
        w2_codes = held.tile([P, S], U32, name="w2_codes", align_bytes=64)
        w2_plane = held.tile([P, S], U8, name="w2_plane", align_bytes=64)
        larger(0, HALF)
        nc.vector.quantize_mx(out=w2_codes[:].bitcast(FP8X4), scales=w2_plane[:], in_=w2_grouped[:])
        signed(0, HALF)
        apply_gate(0, 1)
        quantise_z(0, HALF)
        for t in range(1, PACK):
            apply_gate(t, 1)
        larger(HALF, HALF + Q)
        larger(HALF + Q, S)
        signed(HALF, HALF + Q)
        signed(HALF + Q, S)
        quantise_z(HALF, HALF + Q)
        quantise_z(HALF + Q, S)

        first_banks = [psum.tile([P, 2, HALF], F32, name="first_bank%d" % u) for u in range(2)]
        quarter_banks = [psum.tile([P, Q], F32, name="quarter_bank", tag="bank0_%d" % u) for u in range(2)]

        def product(dst, t, lo, hi):
            cols = slice(t * P, (t + 1) * P)
            nc.tensor.matmul_mx(out=dst, lhsT=w2_codes[:, cols].bitcast(FP8X4), lhsT_scale=w2_plane[:, cols],
                                rhs=z_codes[:, lo:hi].bitcast(FP8X4), rhs_scale=z_plane[:, lo:hi], start=True, stop=True)

        first = [first_banks[t % 2][:, t // 2, :] for t in range(PACK)]
        for t in range(PACK):
            product(first[t], t, 0, HALF)
        for t in range(PACK):
            nc.scalar.activation(size[t][:, :HALF], first[t], ACT.Abs)
        for t in range(PACK):
            nc.scalar.copy(h[t][:, :HALF], first[t])
        for t in range(PACK):
            nc.vector.tensor_copy(size_here[t][:, :HALF], size[t][:, :HALF])
        second = [None]
        for u in range(2):
            product(quarter_banks[u][:], 0, HALF + u * Q, HALF + (u + 1) * Q)
        for t in range(1, PACK):
            bank = psum.tile([P, HALF], F32, name="second_bank", tag="bank%d_0" % t)
            product(bank[:], t, HALF, S)
            second.append(bank)

        def second_pieces(t):
            if t == 0:
                return [(quarter_banks[u][:], slice(HALF + u * Q, HALF + (u + 1) * Q)) for u in range(2)]
            return [(second[t][:], slice(HALF, S))]

        def sizes(t):
            for dst in (size, size_here):
                for src, cols in second_pieces(t):
                    nc.scalar.activation(dst[t][:, cols], src, ACT.Abs)

        total = [held.tile([P, S], F32, name="total%d" % t) for t in range(PACK)]
        root = [held.tile([P, S], F32, name="root%d" % t) for t in range(PACK)]
        inverse = [held.tile([P, S], F32, name="inverse%d" % t) for t in range(PACK)]
        result = [held.tile([P, S], F32, name="result%d" % t) for t in range(PACK)]
        out_rows = out.rearrange("(p t) c -> p t c", t=PACK)

        def add_sizes(t):
            cuts = [0, HALF, S] if t == 0 else [0, S]
            for lo, hi in zip(cuts, cuts[1:]):
                nc.vector.tensor_tensor(total[t][:, lo:hi], size_window[t][:].indirect(n4_t[:, lo // 16:hi // 16]), size_here[t][:, lo:hi], ALU.add)

        def last_cuts(t):
            cuts = [0, S - Q, S] if t == PACK - 1 else [0, S]
            return list(zip(cuts, cuts[1:]))

        def invert(t):
            for lo, hi in last_cuts(t):
                nc.scalar.activation(root[t][:, lo:hi], total[t][:, lo:hi], ACT.Abs_reciprocal_sqrt, bias=0.5)
            for src, cols in second_pieces(t):
                nc.scalar.copy(h[t][:, cols], src)
            for lo, hi in last_cuts(t):
                nc.scalar.activation(inverse[t][:, lo:hi], root[t][:, lo:hi], ACT.Square)

        def finish(t):
            for lo, hi in last_cuts(t):
                nc.vector.tensor_tensor(result[t][:, lo:hi], h_window[t][:].indirect(n3_t[:, lo // 16:hi // 16]), inverse[t][:, lo:hi], ALU.mult)
                (nc.scalar if lo > 0 else nc.sync).dma_start(out_rows[:, t, lo:hi], result[t][:, lo:hi])

        for t in range(PACK - 1):
            sizes(t)
            add_sizes(t)
        invert(0)
        finish(0)
        sizes(PACK - 1)
        add_sizes(PACK - 1)
        for t in range(1, PACK):
            invert(t)
            finish(t)
